import numpy as np
import ml_dtypes


def mxq(x, axis, fmt="e4m3"):
    dtype, down = {"e4m3": (ml_dtypes.float8_e4m3fn, 7), "e5m2": (ml_dtypes.float8_e5m2, 14)}[fmt]
    v = np.moveaxis(np.asarray(x, np.float32).astype(ml_dtypes.bfloat16).astype(np.float64), axis, -1)
    blocks = v.reshape(v.shape[:-1] + (-1, 32))
    amax = np.abs(blocks).max(-1, keepdims=True)
    byte = np.maximum(np.where(amax > 0, np.frexp(amax)[1] - 1 + 127, 0) - down, 1)
    scale = np.exp2(byte - 127.0)
    codes = (blocks / scale).astype(np.float32).astype(dtype).astype(np.float64)
    return np.moveaxis((codes * scale).reshape(v.shape), -1, axis)


WIDE = False


def mx_kscale(k):
    if not WIDE:
        return np.ones(k)
    levels = np.array([10, -10, 5, -5, 0])
    if k % 512:
        return np.exp2(np.random.permutation(np.resize(levels, k // 32))).repeat(32)
    a = np.empty((k // 512, 16))
    for p in range(k // 512):
        a[p, :8] = np.random.permutation(np.resize(levels, 8))
        for g in range(8):
            far = levels[np.abs(levels - a[p, g]) >= 10]
            a[p, g + 8] = far[np.random.randint(len(far))]
    return np.exp2(a.ravel()).repeat(32)


def f64(x):
    return np.asarray(x).astype(np.float64)


def striped(idx):
    return np.tile(idx.reshape(-1, 16).T, (8, 1)).astype(np.uint16)


def unstriped(offs):
    return offs[:16].T.reshape(-1).astype(np.int64)


E2M1 = np.array([0.0, 0.5, 1.0, 1.5, 2.0, 3.0, 4.0, 6.0, -0.0, -0.5, -1.0, -1.5, -2.0, -3.0, -4.0, -6.0])


def pack_weight(w, fmt):
    k, n = w.shape
    w = f64(np.asarray(w, np.float32).astype(ml_dtypes.bfloat16)).reshape(k // 32, 32, n)
    amax = np.abs(w).max(1)
    if fmt == "e4m3":
        byte = np.frexp(amax)[1] - 1 + 127 - 7
    else:
        mant, ex = np.frexp(amax / 6.0)
        byte = np.where(mant > 0.5, ex, ex - 1) + 127
    byte = np.clip(np.where(amax > 0, byte, 1), 1, 254)
    scaled = (w * np.exp2(127.0 - byte)[:, None, :]).reshape(k, n).astype(np.float32)
    by_word = np.ascontiguousarray(scaled.reshape(k // 512, 128, 4, n).transpose(0, 1, 3, 2))
    if fmt == "e4m3":
        words = by_word.astype(ml_dtypes.float8_e4m3fn).view(np.uint8)
    else:
        c = by_word.astype(ml_dtypes.float4_e2m1fn).view(np.uint8) & 0xF
        words = (c[..., 0::2] | (c[..., 1::2] << 4)).reshape(k // 512, 128, 2 * n)
    return np.ascontiguousarray(words), np.ascontiguousarray(byte.astype(np.uint8).reshape(k // 512, 16, n))


def unpack_weight(words, scales, fmt):
    g, _, n = scales.shape
    words = np.ascontiguousarray(words).reshape(g, 128, n, -1)
    if fmt == "e4m3":
        vals = words.view(ml_dtypes.float8_e4m3fn).astype(np.float64)
    else:
        nib = np.empty((g, 128, n, 4), np.uint8)
        nib[..., 0::2] = words & 0xF
        nib[..., 1::2] = words >> 4
        vals = E2M1[nib]
    vals = vals * np.repeat(np.exp2(scales.astype(np.float64) - 127.0), 8, axis=1)[..., None]
    return vals.transpose(0, 1, 3, 2).reshape(g * 512, n)


def gelu(v):
    return 0.5 * v * (1.0 + np.tanh(np.sqrt(2.0 / np.pi) * (v + 0.044715 * v**3)))


K, H, T, S, T2, T3, S2, P = 1024, 1024, 2048, 1024, 2048, 2048, 1024, 512

def setup_inputs():
    n = np.random.standard_normal
    s = mx_kscale(K)[:, None]
    u = mx_kscale(H)[:, None]
    tab_words, tab_scales = pack_weight(n((K, T)) * s, "e4m3")
    tab2_words, tab2_scales = pack_weight(n((H, T3)) / np.sqrt(H) / u, "e4m3")
    w2_words, w2_scales = pack_weight(1.4 * n((H, H)) / np.sqrt(H) / u, "e2m1")
    return {
        "tab_words": tab_words, "tab_scales": tab_scales,
        "tab2_words": tab2_words, "tab2_scales": tab2_scales,
        "offs": striped(np.random.permutation(T)[:S]),
        "offs2": striped(np.random.permutation(T3)[:S2]),
        "offs3": striped(np.random.permutation(T2)[:S]),
        "offs4": striped(np.random.permutation(T2)[:P]),
        "w1": (1.3 * n((K, H)) / np.sqrt(K) / s).astype(np.float32),
        "b1": (0.5 * n(H)).astype(np.float32),
        "gd": (np.exp(0.3 * n(H)) * u[:, 0]).astype(np.float32),
        "w2_words": w2_words, "w2_scales": w2_scales,
        "wgs": np.exp(0.3 * n((128, S))).astype(np.float32),
        "page0": (0.8 * n((H, T2)) * u).astype(np.float32),
        "gx": np.exp(0.3 * n(H)).astype(np.float32),
        "topo": (0.7 * n((S2, P))).astype(np.float32),
    }

def reference(tab_words, tab_scales, tab2_words, tab2_scales, offs, offs2, offs3, offs4,
              w1, b1, gd, w2_words, w2_scales, wgs, page0, gx, topo):
    v = unpack_weight(tab_words, tab_scales, "e4m3")[:, unstriped(offs)]
    v2 = unpack_weight(tab2_words, tab2_scales, "e4m3")[:, unstriped(offs2)]
    w2 = unpack_weight(w2_words, w2_scales, "e2m1")
    y1 = mxq(f64(w1), 0, "e4m3").T @ v
    d = np.tanh(y1 + f64(b1)[:, None]) * f64(gd)[:, None]
    h = d * (w2.T @ mxq(d, 0, "e4m3"))
    page = f64(page0).copy()
    page[:, unstriped(offs3)] = np.tile(f64(wgs), (H // 128, 1)) * h
    x = page[:, unstriped(offs4)] * f64(gx)[:, None]
    e = v2.T @ mxq(x, 0, "e4m3")
    return e + f64(topo)

@@ -1,0 +1,334 @@
+from contextlib import ExitStack
+
+import concourse.mybir as mybir
+
+K, H, T, S, T2, T3, S2, NP = 1024, 1024, 2048, 1024, 2048, 2048, 1024, 512
+FLOPS = 2 * K * H * S + 2 * H * H * S + 2 * H * S2 * NP
+
+F32 = mybir.dt.float32
+BF16 = mybir.dt.bfloat16
+I32 = mybir.dt.int32
+U32 = mybir.dt.uint32
+U16 = mybir.dt.uint16
+U8 = mybir.dt.uint8
+FP8X4 = mybir.dt.float8_e4m3fn_x4
+FP4X4 = mybir.dt.float4_e2m1fn_x4
+MULT = mybir.AluOpType.mult
+ADD = mybir.AluOpType.add
+COPY = mybir.ActivationFunctionType.Copy
+TANH = mybir.ActivationFunctionType.Tanh
+
+P = 128
+PACK = 4
+KP = P * PACK
+PASSES = 2
+CHUNKS = ((0, 256), (256, 256), (512, 512))
+
+
+def tile_list_log_cause_scores_kernel(
+    tc, tab_words, tab_scales, tab2_words, tab2_scales, offs, offs2, offs3, offs4,
+    w1, b1, gd, w2_words, w2_scales, wgs, page0, gx, topo, out,
+):
+    nc = tc.nc
+    with ExitStack() as ctx:
+        keep = ctx.enter_context(tc.tile_pool(name="keep", bufs=1))
+        ring = ctx.enter_context(tc.tile_pool(name="ring", bufs=1))
+        psum = ctx.enter_context(tc.psum_pool(name="psum", bufs=1))
+
+        def kept(shape, dtype, name):
+            return keep.tile(shape, dtype, name=name, align_bytes=64)
+
+        def shared(shape, dtype, name, tag, bufs=1):
+            return ring.tile(shape, dtype, name=name, tag=tag, bufs=bufs, align_bytes=64)
+
+        o1 = keep.tile([P, S // 16], U16, name="o1")
+        o2 = keep.tile([P, S2 // 16], U16, name="o2")
+        o3 = keep.tile([P, S // 16], U16, name="o3")
+        o4 = keep.tile([P, NP // 16], U16, name="o4")
+
+        tab_s = kept([P, T], U8, "tab_s")
+        tab2_s = kept([P, T3], U8, "tab2_s")
+        w2_s_raw = shared([P, PASSES, H], U8, "w2_s_raw", "picked", bufs=3)
+        nc.vector.memset(tab_s[:].bitcast(I32), 0)
+        nc.vector.memset(tab2_s[:].bitcast(I32), 0)
+        nc.vector.memset(w2_s_raw[:].rearrange("p g n -> p (g n)").bitcast(I32), 0)
+
+        def load_table_scales(queue, tile, src):
+            for q in range(4):
+                queue.dma_start(
+                    out=tile[32 * q : 32 * q + 4 * PASSES, :].bitcast(I32),
+                    in_=src[:, 4 * q : 4 * q + 4, :].bitcast(I32),
+                )
+
+        def load_words(src, g, name, tag):
+            t = shared([P, T], I32, name, tag)
+            nc.sync.dma_start(out=t[:], in_=src[g].rearrange("p t i -> p (t i)").bitcast(I32))
+            return t
+
+        def load_w1(a, g):
+            t = shared([P, PACK, KP], F32, "w1raw%d%d" % (a, g), "big%d" % (2 * a + g))
+            rows = w1[KP * g : KP * (g + 1), KP * a : KP * (a + 1)]
+            nc.sync.dma_start(out=t[:], in_=rows.rearrange("(p j) c -> p j c", j=PACK))
+            return t
+
+        def load_vec(src, name):
+            t = kept([P, PASSES, PACK], F32, name)
+            nc.gpsimd.dma_start(out=t[:], in_=src.rearrange("(a p i) -> p a i", a=PASSES, i=PACK))
+            return t
+
+        def load_wgs(c0, n, name):
+            t = kept([P, PACK, n], F32, name)
+            for q in (0, 2, 1, 3):
+                nc.sync.dma_start(
+                    out=t[32 * q : 32 * q + 32, :, :],
+                    in_=wgs[:, c0 : c0 + n].rearrange("(p i) j -> p i j", i=PACK),
+                )
+            return t
+
+        page_rows = page0.rearrange("(a p i) c -> a i p c", a=PASSES, i=PACK)
+
+        def load_page(k):
+            tag = "page%d" % k if k < 6 else "words%d" % (k - 6)
+            t = shared([P, T2], F32, "page%d" % k, tag)
+            nc.sync.dma_start(out=t[:], in_=page_rows[k // PACK, k % PACK])
+            return t
+
+        nc.sync.dma_start(o1[:], offs)
+        load_table_scales(nc.sync, tab_s, tab_scales)
+        tabw = {}
+        w1raw = {}
+        tabw[0] = load_words(tab_words, 0, "tabw0", "words0")
+        w1raw[0, 0] = load_w1(0, 0)
+        nc.sync.dma_start(o2[:], offs2)
+        tabw[1] = load_words(tab_words, 1, "tabw1", "words1")
+        w1raw[0, 1] = load_w1(0, 1)
+        w2_raw = shared([P, PASSES, 2 * H], U8, "w2_raw", "dg10")
+        nc.sync.dma_start(
+            out=w2_raw[:].bitcast(I32), in_=w2_words.rearrange("g p n -> p g n").bitcast(I32)
+        )
+        w1raw[1, 0] = load_w1(1, 0)
+        w1raw[1, 1] = load_w1(1, 1)
+        tab2w = {}
+        tab2w[0] = load_words(tab2_words, 0, "tab2w0", "words2")
+        nc.sync.dma_start(o3[:], offs3)
+        wgs_sb = [load_wgs(CHUNKS[0][0], CHUNKS[0][1], "wgs0")]
+        pages = [load_page(k) for k in range(6)]
+
+        def load_topo(half):
+            t = shared([P, 4, NP], F32, "topo%d" % half, "words%d" % (2 + half))
+            nc.sync.dma_start(
+                out=t[:], in_=topo[KP * half : KP * (half + 1), :].rearrange("(t p) j -> p t j", p=P)
+            )
+            return t
+
+        load_table_scales(nc.gpsimd, tab2_s, tab2_scales)
+        for q in range(4):
+            nc.gpsimd.dma_start(
+                out=w2_s_raw[32 * q : 32 * q + 4, :, :].bitcast(I32),
+                in_=w2_scales[:, 4 * q : 4 * q + 4, :].rearrange("g r n -> r g n").bitcast(I32),
+            )
+        b1_sb = load_vec(b1, "b1_sb")
+        gd_sb = load_vec(gd, "gd_sb")
+        gx_sb = load_vec(gx, "gx_sb")
+
+        v_s = kept([P, S], U8, "v_s")
+        v2_s = kept([P, S2], U8, "v2_s")
+        v_w = [kept([P, S], U32, "v_w%d" % g) for g in range(PASSES)]
+        v2_w = [kept([P, S2], U32, "v2_w%d" % g) for g in range(PASSES)]
+
+        def gather_words(dst, src, o):
+            nc.vector.tensor_copy(dst[:], src[:].bitcast(U32).indirect(o[:]))
+
+        w1_c = {}
+        w1_s = {}
+
+        def prepare_w1(a, g, engine):
+            wb = shared([P, PACK, P, PACK], BF16, "w1bf%d%d" % (a, g), "bf", bufs=2)
+            dst = wb[:].rearrange("p t m j -> p m j t")
+            srcv = w1raw[a, g][:].rearrange("p j (m t) -> p m j t", t=PACK)
+            if engine == "scalar":
+                nc.scalar.copy(out=dst, in_=srcv)
+            else:
+                nc.vector.tensor_copy(out=dst, in_=srcv)
+            w1_c[a, g] = shared([P, KP], U32, "w1c%d%d" % (a, g), "code%d" % (2 * a + g))
+            w1_s[a, g] = kept([P, KP], U8, "w1s%d%d" % (a, g))
+            nc.vector.quantize_mx(
+                out=w1_c[a, g][:].bitcast(FP8X4),
+                scales=w1_s[a, g][:],
+                in_=wb[:].rearrange("p t m j -> p (t m j)"),
+            )
+
+        nc.vector.tensor_copy(v_s[:], tab_s[:].indirect(o1[:]))
+        gather_words(v_w[0], tabw[0], o1)
+        prepare_w1(0, 0, "scalar")
+        gather_words(v_w[1], tabw[1], o1)
+        pages.extend([load_page(6), load_page(7)])
+        wgs_sb.append(load_wgs(CHUNKS[1][0], CHUNKS[1][1], "wgs1"))
+        tab2w[1] = load_words(tab2_words, 1, "tab2w1", "words3")
+        wgs_sb.append(load_wgs(CHUNKS[2][0], CHUNKS[2][1], "wgs2"))
+        nc.sync.dma_start(o4[:], offs4)
+        prepare_w1(0, 1, "scalar")
+        prepare_w1(1, 0, "scalar")
+        prepare_w1(1, 1, "vector")
+
+        w2_c = kept([P, PASSES, PASSES, PACK, P, 2], U8, "w2_c")
+        w2_s = kept([P, PASSES, PASSES, PACK, P], U8, "w2_s")
+        nc.vector.tensor_copy(
+            out=w2_s[:].rearrange("p g a i m -> p (g a) m i"),
+            in_=w2_s_raw[:].rearrange("p g (a m i) -> p (g a) m i", a=PASSES, i=PACK),
+        )
+        for g in range(PASSES):
+            nc.vector.tensor_copy(
+                out=w2_c[:, g].rearrange("p a i m b -> p a m i b"),
+                in_=w2_raw[:, g, :].rearrange("p (a m i b) -> p a m i b", a=PASSES, i=PACK, b=2),
+            )
+
+        t_sb = {}
+        d_c = {}
+        d_s = {}
+
+        def features(c, a):
+            c0, n = CHUNKS[c]
+            cols = slice(c0, c0 + n)
+            if n == KP:
+                t = shared([P, PACK, n], F32, "t%d%d" % (c, a), "big%d" % a)
+            else:
+                t = kept([P, PACK, n], F32, "t%d%d" % (c, a))
+            t_sb[c, a] = t
+            grouped = shared([P, n, PACK], BF16, "dg%d%d" % (c, a), "dg%d%d" % (n // KP, a), bufs=2 - n // KP)
+            on_vector = c == 0 and a == 1
+            if not on_vector:
+                planes = shared([P, PACK, n], BF16, "dp%d%d" % (c, a), "planes")
+            for i in range(PACK):
+                y1 = psum.tile([P, n], F32, name="y1_%d%d%d" % (c, a, i), tag="acc_a", bufs=3)
+                for g in range(PASSES):
+                    nc.tensor.matmul_mx(
+                        out=y1[:],
+                        lhsT=w1_c[a, g][:, P * i : P * (i + 1)].bitcast(FP8X4),
+                        lhsT_scale=w1_s[a, g][:, P * i : P * (i + 1)],
+                        rhs=v_w[g][:, cols].bitcast(FP8X4),
+                        rhs_scale=v_s[4 * g : P, cols],
+                        start=(g == 0),
+                        stop=(g == PASSES - 1),
+                    )
+                nc.scalar.activation(out=t[:, i, :], in_=y1[:], func=TANH, bias=b1_sb[:, a, i : i + 1])
+                if on_vector:
+                    nc.vector.tensor_scalar(
+                        out=grouped[:, :, i], in0=t[:, i, :], scalar1=gd_sb[:, a, i : i + 1],
+                        scalar2=None, op0=MULT,
+                    )
+                else:
+                    nc.scalar.activation(
+                        out=planes[:, i, :], in_=t[:, i, :], func=COPY, scale=gd_sb[:, a, i : i + 1]
+                    )
+            if not on_vector:
+                nc.scalar.copy(
+                    out=grouped[:].rearrange("p (c e) i -> p c i e", e=4),
+                    in_=planes[:].rearrange("p i (c e) -> p c i e", e=4),
+                )
+            d_c[c, a] = kept([P, n], U32, "dc%d%d" % (c, a))
+            d_s[c, a] = kept([P, n], U8, "ds%d%d" % (c, a))
+            nc.vector.quantize_mx(
+                out=d_c[c, a][:].bitcast(FP8X4),
+                scales=d_s[c, a][:],
+                in_=grouped[:].rearrange("p n i -> p (n i)"),
+            )
+
+        h_sb = {}
+
+        def mixture(c, k):
+            a, i = divmod(k, PACK)
+            c0, n = CHUNKS[c]
+            y2 = psum.tile([P, n], F32, name="y2_%d%d" % (c, k), tag="acc_b", bufs=5)
+            for g in range(PASSES):
+                nc.tensor.matmul_mx(
+                    out=y2[:],
+                    lhsT=w2_c[:, g, a, i].rearrange("p m b -> p (m b)").bitcast(FP4X4),
+                    lhsT_scale=w2_s[:, g, a, i, :],
+                    rhs=d_c[c, g][:].bitcast(FP8X4),
+                    rhs_scale=d_s[c, g][:],
+                    start=(g == 0),
+                    stop=(g == PASSES - 1),
+                )
+            h = shared([P, n], F32, "h%d%d" % (c, k), "h", bufs=3)
+            nc.vector.scalar_tensor_tensor(
+                out=h[:], in0=y2[:], scalar=gd_sb[:, a, i : i + 1], in1=t_sb[c, a][:, i, :],
+                op0=MULT, op1=MULT,
+            )
+            h_sb[c, k] = h
+
+        def put(c, k):
+            i = k % PACK
+            c0, n = CHUNKS[c]
+            w = wgs_sb[c][:, i, :]
+            nc.vector.tensor_tensor(
+                pages[k][:].indirect(o3[:, c0 // 16 : (c0 + n) // 16]), h_sb[c, k][:], w, MULT
+            )
+
+        x_g = {}
+        x_c = {}
+        x_s = {}
+
+        def fetch(k):
+            a, i = divmod(k, PACK)
+            picked = shared([P, NP], F32, "picked%d" % k, "picked", bufs=3)
+            nc.vector.tensor_copy(picked[:], pages[k][:].indirect(o4[:]))
+            if i == 0:
+                x_g[a] = shared([P, NP, PACK], BF16, "xg%d" % a, "dg1%d" % a)
+            nc.scalar.activation(
+                out=x_g[a][:, :, i], in_=picked[:], func=COPY, scale=gx_sb[:, a, i : i + 1]
+            )
+
+        def quantise_x(a):
+            x_c[a] = shared([P, NP], U32, "xc%d" % a, "code%d" % a)
+            x_s[a] = kept([P, NP], U8, "xs%d" % a)
+            nc.vector.quantize_mx(
+                out=x_c[a][:].bitcast(FP8X4),
+                scales=x_s[a][:],
+                in_=x_g[a][:].rearrange("p n i -> p (n i)"),
+            )
+
+        nc.vector.tensor_copy(v2_s[:], tab2_s[:].indirect(o2[:]))
+        features(0, 0)
+        features(0, 1)
+        gather_words(v2_w[0], tab2w[0], o2)
+        for c in range(1, len(CHUNKS)):
+            features(c, 0)
+            features(c, 1)
+        steps = [(c, k) for c in range(len(CHUNKS)) for k in range(8)]
+        last = len(CHUNKS) - 1
+        mixture(*steps[0])
+        for s, (c, k) in enumerate(steps):
+            if s + 1 < len(steps):
+                mixture(*steps[s + 1])
+            put(c, k)
+            if s == 10:
+                gather_words(v2_w[1], tab2w[1], o2)
+                topo_sb = [load_topo(0), load_topo(1)]
+            if c == last and k > 0:
+                fetch(k - 1)
+            if c == last and k == PACK + 1:
+                quantise_x(0)
+        fetch(7)
+        quantise_x(1)
+
+        acc = []
+        for m in range(8):
+            tag, bufs = ("acc_a", 3) if m < 3 else ("acc_b", 5)
+            acc.append(psum.tile([P, NP], F32, name="e%d" % m, tag=tag, bufs=bufs))
+        for g in range(PASSES):
+            for m in range(8):
+                nc.tensor.matmul_mx(
+                    out=acc[m][:],
+                    lhsT=v2_w[g][:, P * m : P * (m + 1)].bitcast(FP8X4),
+                    lhsT_scale=v2_s[4 * g : P, P * m : P * (m + 1)],
+                    rhs=x_c[g][:].bitcast(FP8X4),
+                    rhs_scale=x_s[g][:],
+                    start=(g == 0),
+                    stop=(g == PASSES - 1),
+                )
+        res = [shared([P, 4, NP], F32, "res%d" % half, "big%d" % (2 + half)) for half in range(2)]
+        for m in range(8):
+            r = res[m // 4][:, m % 4, :]
+            nc.vector.tensor_tensor(r, acc[m][:], topo_sb[m // 4][:, m % 4, :], ADD)
+            nc.sync.dma_start(out=out[P * m : P * (m + 1), :], in_=r)

@@ -50,8 +50,8 @@ def tile_list_log_cause_scores_kernel(
         tab2_s = kept([P, T3], U8, "tab2_s")
         w2_s_raw = shared([P, PASSES, H], U8, "w2_s_raw", "picked", bufs=3)
         nc.vector.memset(tab_s[:].bitcast(I32), 0)
-        nc.vector.memset(tab2_s[:].bitcast(I32), 0)
         nc.vector.memset(w2_s_raw[:].rearrange("p g n -> p (g n)").bitcast(I32), 0)
+        nc.vector.memset(tab2_s[:].bitcast(I32), 0)
 
         def load_table_scales(queue, tile, src):
             for q in range(4):
@@ -73,7 +73,7 @@ def tile_list_log_cause_scores_kernel(
 
         def load_vec(src, name):
             t = kept([P, PASSES, PACK], F32, name)
-            nc.gpsimd.dma_start(out=t[:], in_=src.rearrange("(a p i) -> p a i", a=PASSES, i=PACK))
+            nc.sync.dma_start(out=t[:], in_=src.rearrange("(a p i) -> p a i", a=PASSES, i=PACK))
             return t
 
         def load_wgs(c0, n, name):
@@ -94,25 +94,37 @@ def tile_list_log_cause_scores_kernel(
             return t
 
         nc.sync.dma_start(o1[:], offs)
-        load_table_scales(nc.sync, tab_s, tab_scales)
+        b1_sb = load_vec(b1, "b1_sb")
+        gd_sb = load_vec(gd, "gd_sb")
+        gx_sb = load_vec(gx, "gx_sb")
+        nc.sync.dma_start(o2[:], offs2)
+        nc.sync.dma_start(o3[:], offs3)
+        nc.sync.dma_start(o4[:], offs4)
         tabw = {}
         w1raw = {}
         tabw[0] = load_words(tab_words, 0, "tabw0", "words0")
+        load_table_scales(nc.sync, tab_s, tab_scales)
         w1raw[0, 0] = load_w1(0, 0)
-        nc.sync.dma_start(o2[:], offs2)
-        tabw[1] = load_words(tab_words, 1, "tabw1", "words1")
-        w1raw[0, 1] = load_w1(0, 1)
         w2_raw = shared([P, PASSES, 2 * H], U8, "w2_raw", "dg10")
         nc.sync.dma_start(
             out=w2_raw[:].bitcast(I32), in_=w2_words.rearrange("g p n -> p g n").bitcast(I32)
         )
+        tabw[1] = load_words(tab_words, 1, "tabw1", "words1")
+        for q in range(4):
+            nc.sync.dma_start(
+                out=w2_s_raw[32 * q : 32 * q + 4, :, :].bitcast(I32),
+                in_=w2_scales[:, 4 * q : 4 * q + 4, :].rearrange("g r n -> r g n").bitcast(I32),
+            )
+        w1raw[0, 1] = load_w1(0, 1)
         w1raw[1, 0] = load_w1(1, 0)
         w1raw[1, 1] = load_w1(1, 1)
+        load_table_scales(nc.sync, tab2_s, tab2_scales)
+        wgs_sb = [load_wgs(CHUNKS[0][0], CHUNKS[0][1], "wgs0")]
         tab2w = {}
         tab2w[0] = load_words(tab2_words, 0, "tab2w0", "words2")
-        nc.sync.dma_start(o3[:], offs3)
-        wgs_sb = [load_wgs(CHUNKS[0][0], CHUNKS[0][1], "wgs0")]
-        pages = [load_page(k) for k in range(6)]
+        pages = [load_page(k) for k in range(4)]
+        wgs_sb.append(load_wgs(CHUNKS[1][0], CHUNKS[1][1], "wgs1"))
+        pages.extend([load_page(4), load_page(5)])
 
         def load_topo(half):
             t = shared([P, 4, NP], F32, "topo%d" % half, "words%d" % (2 + half))
@@ -121,20 +133,9 @@ def tile_list_log_cause_scores_kernel(
             )
             return t
 
-        load_table_scales(nc.gpsimd, tab2_s, tab2_scales)
-        for q in range(4):
-            nc.gpsimd.dma_start(
-                out=w2_s_raw[32 * q : 32 * q + 4, :, :].bitcast(I32),
-                in_=w2_scales[:, 4 * q : 4 * q + 4, :].rearrange("g r n -> r g n").bitcast(I32),
-            )
-        b1_sb = load_vec(b1, "b1_sb")
-        gd_sb = load_vec(gd, "gd_sb")
-        gx_sb = load_vec(gx, "gx_sb")
-
         v_s = kept([P, S], U8, "v_s")
-        v2_s = kept([P, S2], U8, "v2_s")
         v_w = [kept([P, S], U32, "v_w%d" % g) for g in range(PASSES)]
-        v2_w = [kept([P, S2], U32, "v2_w%d" % g) for g in range(PASSES)]
+        v2_w = {1: kept([P, S2], U32, "v2_w1")}
 
         def gather_words(dst, src, o):
             nc.vector.tensor_copy(dst[:], src[:].bitcast(U32).indirect(o[:]))
@@ -143,7 +144,7 @@ def tile_list_log_cause_scores_kernel(
         w1_s = {}
 
         def prepare_w1(a, g, engine):
-            wb = shared([P, PACK, P, PACK], BF16, "w1bf%d%d" % (a, g), "bf", bufs=2)
+            wb = shared([P, PACK, P, PACK], BF16, "w1bf%d%d" % (a, g), "bf%d" % g)
             dst = wb[:].rearrange("p t m j -> p m j t")
             srcv = w1raw[a, g][:].rearrange("p j (m t) -> p m j t", t=PACK)
             if engine == "scalar":
@@ -158,30 +159,27 @@ def tile_list_log_cause_scores_kernel(
                 in_=wb[:].rearrange("p t m j -> p (t m j)"),
             )
 
-        nc.vector.tensor_copy(v_s[:], tab_s[:].indirect(o1[:]))
         gather_words(v_w[0], tabw[0], o1)
+        nc.vector.tensor_copy(v_s[:], tab_s[:].indirect(o1[:]))
         prepare_w1(0, 0, "scalar")
+        w2_c = kept([P, PASSES, PASSES, PACK, P], U16, "w2_c")
+        nc.scalar.copy(
+            out=w2_c[:].rearrange("p g a i m -> p (g a) m i"),
+            in_=w2_raw[:].rearrange("p g n -> p (g n)").bitcast(U16).rearrange("p (q m i) -> p q m i", m=P, i=PACK),
+        )
         gather_words(v_w[1], tabw[1], o1)
         pages.extend([load_page(6), load_page(7)])
-        wgs_sb.append(load_wgs(CHUNKS[1][0], CHUNKS[1][1], "wgs1"))
-        tab2w[1] = load_words(tab2_words, 1, "tab2w1", "words3")
         wgs_sb.append(load_wgs(CHUNKS[2][0], CHUNKS[2][1], "wgs2"))
-        nc.sync.dma_start(o4[:], offs4)
+        tab2w[1] = load_words(tab2_words, 1, "tab2w1", "words3")
         prepare_w1(0, 1, "scalar")
-        prepare_w1(1, 0, "scalar")
-        prepare_w1(1, 1, "vector")
-
-        w2_c = kept([P, PASSES, PASSES, PACK, P, 2], U8, "w2_c")
         w2_s = kept([P, PASSES, PASSES, PACK, P], U8, "w2_s")
         nc.vector.tensor_copy(
             out=w2_s[:].rearrange("p g a i m -> p (g a) m i"),
             in_=w2_s_raw[:].rearrange("p g (a m i) -> p (g a) m i", a=PASSES, i=PACK),
         )
-        for g in range(PASSES):
-            nc.vector.tensor_copy(
-                out=w2_c[:, g].rearrange("p a i m b -> p a m i b"),
-                in_=w2_raw[:, g, :].rearrange("p (a m i b) -> p a m i b", a=PASSES, i=PACK, b=2),
-            )
+
+        prepare_w1(1, 0, "scalar")
+        prepare_w1(1, 1, "vector")
 
         t_sb = {}
         d_c = {}
@@ -190,12 +188,12 @@ def tile_list_log_cause_scores_kernel(
         def features(c, a):
             c0, n = CHUNKS[c]
             cols = slice(c0, c0 + n)
-            if n == KP:
+            if c == 2:
                 t = shared([P, PACK, n], F32, "t%d%d" % (c, a), "big%d" % a)
             else:
                 t = kept([P, PACK, n], F32, "t%d%d" % (c, a))
             t_sb[c, a] = t
-            grouped = shared([P, n, PACK], BF16, "dg%d%d" % (c, a), "dg%d%d" % (n // KP, a), bufs=2 - n // KP)
+            grouped = shared([P, n, PACK], BF16, "dg%d%d" % (c, a), "dg%d%d" % ((c + 2) % 3, a))
             on_vector = c == 0 and a == 1
             if not on_vector:
                 planes = shared([P, PACK, n], BF16, "dp%d%d" % (c, a), "planes")
@@ -243,92 +241,103 @@ def tile_list_log_cause_scores_kernel(
             for g in range(PASSES):
                 nc.tensor.matmul_mx(
                     out=y2[:],
-                    lhsT=w2_c[:, g, a, i].rearrange("p m b -> p (m b)").bitcast(FP4X4),
+                    lhsT=w2_c[:, g, a, i, :].bitcast(FP4X4),
                     lhsT_scale=w2_s[:, g, a, i, :],
                     rhs=d_c[c, g][:].bitcast(FP8X4),
                     rhs_scale=d_s[c, g][:],
                     start=(g == 0),
                     stop=(g == PASSES - 1),
                 )
-            h = shared([P, n], F32, "h%d%d" % (c, k), "h", bufs=3)
-            nc.vector.scalar_tensor_tensor(
-                out=h[:], in0=y2[:], scalar=gd_sb[:, a, i : i + 1], in1=t_sb[c, a][:, i, :],
-                op0=MULT, op1=MULT,
-            )
+            gained = shared([P, n], F32, "h%d%d" % (c, k), "h", bufs=4)
+            nc.scalar.activation(out=gained[:], in_=y2[:], func=COPY, scale=gd_sb[:, a, i : i + 1])
+            h = t_sb[c, a][:, i, :]
+            nc.gpsimd.tensor_tensor(h, h, wgs_sb[c][:, i, :], MULT)
+            nc.gpsimd.tensor_tensor(h, h, gained[:], MULT)
             h_sb[c, k] = h
 
         def put(c, k):
-            i = k % PACK
             c0, n = CHUNKS[c]
-            w = wgs_sb[c][:, i, :]
-            nc.vector.tensor_tensor(
-                pages[k][:].indirect(o3[:, c0 // 16 : (c0 + n) // 16]), h_sb[c, k][:], w, MULT
-            )
+            nc.vector.tensor_copy(pages[k][:].indirect(o3[:, c0 // 16 : (c0 + n) // 16]), h_sb[c, k])
 
         x_g = {}
         x_c = {}
         x_s = {}
 
-        def fetch(k):
+        def fetch(k, j0, n):
             a, i = divmod(k, PACK)
-            picked = shared([P, NP], F32, "picked%d" % k, "picked", bufs=3)
-            nc.vector.tensor_copy(picked[:], pages[k][:].indirect(o4[:]))
-            if i == 0:
+            picked = shared([P, n], F32, "picked%d_%d" % (k, j0), "picked", bufs=3)
+            nc.vector.tensor_copy(picked[:], pages[k][:].indirect(o4[:, j0 // 16 : (j0 + n) // 16]))
+            if a not in x_g:
                 x_g[a] = shared([P, NP, PACK], BF16, "xg%d" % a, "dg1%d" % a)
+                x_c[a] = shared([P, NP], U32, "xc%d" % a, "code%d" % a)
+                x_s[a] = kept([P, NP], U8, "xs%d" % a)
             nc.scalar.activation(
-                out=x_g[a][:, :, i], in_=picked[:], func=COPY, scale=gx_sb[:, a, i : i + 1]
+                out=x_g[a][:, j0 : j0 + n, i], in_=picked[:], func=COPY, scale=gx_sb[:, a, i : i + 1]
             )
 
-        def quantise_x(a):
-            x_c[a] = shared([P, NP], U32, "xc%d" % a, "code%d" % a)
-            x_s[a] = kept([P, NP], U8, "xs%d" % a)
+        def quantise_x(a, j0, n):
             nc.vector.quantize_mx(
-                out=x_c[a][:].bitcast(FP8X4),
-                scales=x_s[a][:],
-                in_=x_g[a][:].rearrange("p n i -> p (n i)"),
+                out=x_c[a][:, j0 : j0 + n].bitcast(FP8X4),
+                scales=x_s[a][:, j0 : j0 + n],
+                in_=x_g[a][:, j0 : j0 + n, :].rearrange("p n i -> p (n i)"),
             )
 
-        nc.vector.tensor_copy(v2_s[:], tab2_s[:].indirect(o2[:]))
         features(0, 0)
         features(0, 1)
+        v2_s = shared([P, S2], U8, "v2_s", "bf1")
+        nc.vector.tensor_copy(v2_s[:], tab2_s[:].indirect(o2[:]))
+        v2_w[0] = shared([P, S2], U32, "v2_w0", "dg21")
         gather_words(v2_w[0], tab2w[0], o2)
-        for c in range(1, len(CHUNKS)):
-            features(c, 0)
-            features(c, 1)
-        steps = [(c, k) for c in range(len(CHUNKS)) for k in range(8)]
+        steps = [(c, k) for half in range(2) for c in range(2) for k in range(PACK * half, PACK * (half + 1))]
+        steps.extend([(c, k) for c in range(2, len(CHUNKS)) for k in range(8)])
         last = len(CHUNKS) - 1
-        mixture(*steps[0])
         for s, (c, k) in enumerate(steps):
-            if s + 1 < len(steps):
-                mixture(*steps[s + 1])
+            if c > 0 and k == 0:
+                features(c, 0)
+                features(c, 1)
+            mixture(c, k)
             put(c, k)
-            if s == 10:
+            if s == 16:
                 gather_words(v2_w[1], tab2w[1], o2)
                 topo_sb = [load_topo(0), load_topo(1)]
             if c == last and k > 0:
-                fetch(k - 1)
+                fetch(k - 1, 0, NP)
             if c == last and k == PACK + 1:
-                quantise_x(0)
-        fetch(7)
-        quantise_x(1)
+                quantise_x(0, 0, NP)
+        half_p = NP // 2
+        for jh in range(2):
+            fetch(7, half_p * jh, half_p)
+        for jh in range(2):
+            quantise_x(1, half_p * jh, half_p)
 
-        acc = []
-        for m in range(8):
-            tag, bufs = ("acc_a", 3) if m < 3 else ("acc_b", 5)
-            acc.append(psum.tile([P, NP], F32, name="e%d" % m, tag=tag, bufs=bufs))
+        banks = [(jh, mp) for jh in range(2) for mp in range(4)]
+        acc = {}
+        for b, key in enumerate(banks):
+            tag, bufs = ("acc_a", 3) if b < 3 else ("acc_b", 5)
+            acc[key] = psum.tile([P, 2, half_p], F32, name="e%d" % b, tag=tag, bufs=bufs)
         for g in range(PASSES):
-            for m in range(8):
-                nc.tensor.matmul_mx(
-                    out=acc[m][:],
-                    lhsT=v2_w[g][:, P * m : P * (m + 1)].bitcast(FP8X4),
-                    lhsT_scale=v2_s[4 * g : P, P * m : P * (m + 1)],
-                    rhs=x_c[g][:].bitcast(FP8X4),
-                    rhs_scale=x_s[g][:],
-                    start=(g == 0),
-                    stop=(g == PASSES - 1),
-                )
-        res = [shared([P, 4, NP], F32, "res%d" % half, "big%d" % (2 + half)) for half in range(2)]
-        for m in range(8):
-            r = res[m // 4][:, m % 4, :]
-            nc.vector.tensor_tensor(r, acc[m][:], topo_sb[m // 4][:, m % 4, :], ADD)
-            nc.sync.dma_start(out=out[P * m : P * (m + 1), :], in_=r)
+            for jh, mp in banks:
+                cols = slice(half_p * jh, half_p * (jh + 1))
+                for u in range(2):
+                    m = 2 * mp + u
+                    nc.tensor.matmul_mx(
+                        out=acc[jh, mp][:, u, :],
+                        lhsT=v2_w[g][:, P * m : P * (m + 1)].bitcast(FP8X4),
+                        lhsT_scale=v2_s[4 * g : P, P * m : P * (m + 1)],
+                        rhs=x_c[g][:, cols].bitcast(FP8X4),
+                        rhs_scale=x_s[g][:, cols],
+                        start=(g == 0 and u == 0),
+                        stop=(g == PASSES - 1 and u == 1),
+                    )
+        res = [shared([P, 4, 2, half_p], F32, "res%d" % jh, "big%d" % (2 + jh)) for jh in range(2)]
+        out_rows = out.rearrange("(t p) j -> p t j", p=P)
+        for jh, mp in banks:
+            cols = slice(half_p * jh, half_p * (jh + 1))
+            r = res[jh][:, mp, :, :]
+            given = topo_sb[mp // 2][:, 2 * (mp % 2) : 2 * (mp % 2) + 2, cols]
+            if jh == 0 and mp % 2 == 1:
+                nc.scalar.copy(out=r, in_=acc[jh, mp][:])
+                nc.gpsimd.tensor_tensor(r, r, given, ADD)
+            else:
+                nc.vector.tensor_tensor(r, acc[jh, mp][:], given, ADD)
+            nc.sync.dma_start(out=out_rows[:, 2 * mp : 2 * mp + 2, cols], in_=r)

@@ -22,7 +22,17 @@ P = 128
 PACK = 4
 KP = P * PACK
 PASSES = 2
+ROW_TILES = PASSES * PACK
+QUADRANTS = 4
+LIST_GROUP = 16
+
 CHUNKS = ((0, 256), (256, 256), (512, 512))
+QUANTISE_AFTER = {(0, 3): (1, 0), (0, 5): (1, 1), (1, 2): (2, 0), (1, 5): (2, 1)}
+GATHER_AFTER = (1, 3)
+FIRST_BANKS = 3
+SECOND_BANKS = 5
+RING = 3
+OWN_PAGE_BUFFERS = 6
 
 
 def tile_list_log_cause_scores_kernel(
@@ -41,164 +51,183 @@ def tile_list_log_cause_scores_kernel(
         def shared(shape, dtype, name, tag, bufs=1):
             return ring.tile(shape, dtype, name=name, tag=tag, bufs=bufs, align_bytes=64)
 
-        o1 = keep.tile([P, S // 16], U16, name="o1")
-        o2 = keep.tile([P, S2 // 16], U16, name="o2")
-        o3 = keep.tile([P, S // 16], U16, name="o3")
-        o4 = keep.tile([P, NP // 16], U16, name="o4")
+        def first_bank(shape, name):
+            return psum.tile(shape, F32, name=name, tag="acc_a", bufs=FIRST_BANKS)
+
+        def second_bank(shape, name):
+            return psum.tile(shape, F32, name=name, tag="acc_b", bufs=SECOND_BANKS)
+
+        idx = keep.tile([P, S // LIST_GROUP], U16, name="idx")
+        idx2 = keep.tile([P, S2 // LIST_GROUP], U16, name="idx2")
+        idx3 = keep.tile([P, S // LIST_GROUP], U16, name="idx3")
+        idx4 = keep.tile([P, NP // LIST_GROUP], U16, name="idx4")
+
+        def entries(list_tile, j0, n):
+            return list_tile[:, j0 // LIST_GROUP : (j0 + n) // LIST_GROUP]
 
         tab_s = kept([P, T], U8, "tab_s")
         tab2_s = kept([P, T3], U8, "tab2_s")
-        w2_s_raw = shared([P, PASSES, H], U8, "w2_s_raw", "picked", bufs=3)
-        nc.vector.memset(tab_s[:].bitcast(I32), 0)
+        w2_s_raw = shared([P, PASSES, H], U8, "w2_s_raw", "picked", bufs=RING)
+        nc.gpsimd.memset(tab_s[:].bitcast(I32), 0)
         nc.vector.memset(w2_s_raw[:].rearrange("p g n -> p (g n)").bitcast(I32), 0)
         nc.vector.memset(tab2_s[:].bitcast(I32), 0)
 
-        def load_table_scales(queue, tile, src):
-            for q in range(4):
-                queue.dma_start(
+        def load_table_scales(tile, src, quadrants):
+            for q in quadrants:
+                nc.sync.dma_start(
                     out=tile[32 * q : 32 * q + 4 * PASSES, :].bitcast(I32),
                     in_=src[:, 4 * q : 4 * q + 4, :].bitcast(I32),
                 )
 
         def load_words(src, g, name, tag):
-            t = shared([P, T], I32, name, tag)
-            nc.sync.dma_start(out=t[:], in_=src[g].rearrange("p t i -> p (t i)").bitcast(I32))
-            return t
+            words = shared([P, T], I32, name, tag)
+            nc.sync.dma_start(out=words[:], in_=src[g].rearrange("p t i -> p (t i)").bitcast(I32))
+            return words
 
-        def load_w1(a, g):
-            t = shared([P, PACK, KP], F32, "w1raw%d%d" % (a, g), "big%d" % (2 * a + g))
-            rows = w1[KP * g : KP * (g + 1), KP * a : KP * (a + 1)]
-            nc.sync.dma_start(out=t[:], in_=rows.rearrange("(p j) c -> p j c", j=PACK))
-            return t
+        def load_w1(g, c0, width, tag):
+            raw = shared([P, PACK, width], F32, "w1raw%d_%d" % (g, c0), tag)
+            rows = w1[KP * g : KP * (g + 1), c0 : c0 + width]
+            nc.sync.dma_start(out=raw[:], in_=rows.rearrange("(p j) c -> p j c", j=PACK))
+            return raw
 
-        def load_vec(src, name):
-            t = kept([P, PASSES, PACK], F32, name)
-            nc.sync.dma_start(out=t[:], in_=src.rearrange("(a p i) -> p a i", a=PASSES, i=PACK))
-            return t
+        def load_channel_vector(src, name):
+            vec = kept([P, PASSES, PACK], F32, name)
+            nc.sync.dma_start(out=vec[:], in_=src.rearrange("(a p i) -> p a i", a=PASSES, i=PACK))
+            return vec
 
-        def load_wgs(c0, n, name):
-            t = kept([P, PACK, n], F32, name)
-            for q in (0, 2, 1, 3):
+        def load_wgs(c, quadrants):
+            c0, n = CHUNKS[c]
+            for q in quadrants:
                 nc.sync.dma_start(
-                    out=t[32 * q : 32 * q + 32, :, :],
+                    out=wgs_sb[c][32 * q : 32 * q + 32, :, :],
                     in_=wgs[:, c0 : c0 + n].rearrange("(p i) j -> p i j", i=PACK),
                 )
-            return t
 
         page_rows = page0.rearrange("(a p i) c -> a i p c", a=PASSES, i=PACK)
 
         def load_page(k):
-            tag = "page%d" % k if k < 6 else "words%d" % (k - 6)
-            t = shared([P, T2], F32, "page%d" % k, tag)
-            nc.sync.dma_start(out=t[:], in_=page_rows[k // PACK, k % PACK])
-            return t
+            tag = "page%d" % k if k < OWN_PAGE_BUFFERS else "words%d" % (k - OWN_PAGE_BUFFERS)
+            page = shared([P, T2], F32, "page%d" % k, tag)
+            nc.sync.dma_start(out=page[:], in_=page_rows[k // PACK, k % PACK])
+            return page
 
-        nc.sync.dma_start(o1[:], offs)
-        b1_sb = load_vec(b1, "b1_sb")
-        gd_sb = load_vec(gd, "gd_sb")
-        gx_sb = load_vec(gx, "gx_sb")
-        nc.sync.dma_start(o2[:], offs2)
-        nc.sync.dma_start(o3[:], offs3)
-        nc.sync.dma_start(o4[:], offs4)
-        tabw = {}
+        def load_topo(half):
+            rows = shared([P, PACK, NP], F32, "topo%d" % half, "words%d" % (PASSES + half))
+            nc.sync.dma_start(
+                out=rows[:],
+                in_=topo[KP * half : KP * (half + 1), :].rearrange("(t p) j -> p t j", p=P),
+            )
+            return rows
+
+        tab_w = {}
+        tab2_w = {}
         w1raw = {}
-        tabw[0] = load_words(tab_words, 0, "tabw0", "words0")
-        load_table_scales(nc.sync, tab_s, tab_scales)
-        w1raw[0, 0] = load_w1(0, 0)
-        w2_raw = shared([P, PASSES, 2 * H], U8, "w2_raw", "dg10")
-        nc.sync.dma_start(
-            out=w2_raw[:].bitcast(I32), in_=w2_words.rearrange("g p n -> p g n").bitcast(I32)
-        )
-        tabw[1] = load_words(tab_words, 1, "tabw1", "words1")
-        for q in range(4):
+        nc.sync.dma_start(idx[:], offs)
+        tab_w[0] = load_words(tab_words, 0, "tab_w0", "words0")
+        b1_sb = load_channel_vector(b1, "b1_sb")
+        gd_sb = load_channel_vector(gd, "gd_sb")
+        load_table_scales(tab_s, tab_scales, range(QUADRANTS))
+        w1raw[0, 0] = [load_w1(0, 0, KP, "big0")]
+        w1raw[0, 1] = [load_w1(1, 0, KP, "big1")]
+        for q in range(QUADRANTS):
             nc.sync.dma_start(
                 out=w2_s_raw[32 * q : 32 * q + 4, :, :].bitcast(I32),
                 in_=w2_scales[:, 4 * q : 4 * q + 4, :].rearrange("g r n -> r g n").bitcast(I32),
             )
-        w1raw[0, 1] = load_w1(0, 1)
-        w1raw[1, 0] = load_w1(1, 0)
-        w1raw[1, 1] = load_w1(1, 1)
-        load_table_scales(nc.sync, tab2_s, tab2_scales)
-        wgs_sb = [load_wgs(CHUNKS[0][0], CHUNKS[0][1], "wgs0")]
-        tab2w = {}
-        tab2w[0] = load_words(tab2_words, 0, "tab2w0", "words2")
-        pages = [load_page(k) for k in range(4)]
-        wgs_sb.append(load_wgs(CHUNKS[1][0], CHUNKS[1][1], "wgs1"))
-        pages.extend([load_page(4), load_page(5)])
-
-        def load_topo(half):
-            t = shared([P, 4, NP], F32, "topo%d" % half, "words%d" % (2 + half))
-            nc.sync.dma_start(
-                out=t[:], in_=topo[KP * half : KP * (half + 1), :].rearrange("(t p) j -> p t j", p=P)
-            )
-            return t
+        tab_w[1] = load_words(tab_words, 1, "tab_w1", "words1")
+        nc.sync.dma_start(idx2[:], offs2)
+        load_table_scales(tab2_s, tab2_scales, (0, 1))
+        w2_raw = shared([P, PASSES, 2 * H], U8, "w2_raw", "grouped10")
+        nc.sync.dma_start(
+            out=w2_raw[:].bitcast(I32), in_=w2_words.rearrange("g p n -> p g n").bitcast(I32)
+        )
+        load_table_scales(tab2_s, tab2_scales, (2, 3))
+        w1raw[1, 0] = [load_w1(0, KP, KP, "big2")]
+        nc.sync.dma_start(idx3[:], offs3)
+        w1raw[1, 1] = [
+            load_w1(1, KP + u * (KP // 2), KP // 2, tag) for u, tag in enumerate(("big3", "planes"))
+        ]
+        wgs_sb = [kept([P, PACK, n], F32, "wgs%d" % c0) for c0, n in CHUNKS]
+        load_wgs(0, (0, 2))
+        tab2_w[0] = load_words(tab2_words, 0, "tab2_w0", "words2")
+        load_wgs(0, (1, 3))
+        pages = [load_page(k) for k in range(OWN_PAGE_BUFFERS)]
 
         v_s = kept([P, S], U8, "v_s")
         v_w = [kept([P, S], U32, "v_w%d" % g) for g in range(PASSES)]
-        v2_w = {1: kept([P, S2], U32, "v2_w1")}
+        v2_w = {}
 
-        def gather_words(dst, src, o):
-            nc.vector.tensor_copy(dst[:], src[:].bitcast(U32).indirect(o[:]))
+        def gather_words(dst, src, list_tile):
+            nc.vector.tensor_copy(dst[:], src[:].bitcast(U32).indirect(list_tile[:]))
 
         w1_c = {}
         w1_s = {}
 
-        def prepare_w1(a, g, engine):
-            wb = shared([P, PACK, P, PACK], BF16, "w1bf%d%d" % (a, g), "bf%d" % g)
-            dst = wb[:].rearrange("p t m j -> p m j t")
-            srcv = w1raw[a, g][:].rearrange("p j (m t) -> p m j t", t=PACK)
-            if engine == "scalar":
-                nc.scalar.copy(out=dst, in_=srcv)
-            else:
-                nc.vector.tensor_copy(out=dst, in_=srcv)
-            w1_c[a, g] = shared([P, KP], U32, "w1c%d%d" % (a, g), "code%d" % (2 * a + g))
+        def quantise_w1(a, g, cast):
+            dealt = shared([P, PACK, P, PACK], BF16, "w1bf%d%d" % (a, g), "bf%d" % g)
+            walk = dealt[:].rearrange("p i m j -> p m j i")
+            pieces = w1raw[a, g]
+            width = P // len(pieces)
+            for u, raw in enumerate(pieces):
+                cast(
+                    out=walk[:, u * width : (u + 1) * width],
+                    in_=raw[:].rearrange("p j (m i) -> p m j i", i=PACK),
+                )
+            w1_c[a, g] = shared([P, KP], U32, "w1c%d%d" % (a, g), "code%d" % (PASSES * a + g))
             w1_s[a, g] = kept([P, KP], U8, "w1s%d%d" % (a, g))
             nc.vector.quantize_mx(
                 out=w1_c[a, g][:].bitcast(FP8X4),
                 scales=w1_s[a, g][:],
-                in_=wb[:].rearrange("p t m j -> p (t m j)"),
+                in_=dealt[:].rearrange("p i m j -> p (i m j)"),
             )
 
-        gather_words(v_w[0], tabw[0], o1)
-        nc.vector.tensor_copy(v_s[:], tab_s[:].indirect(o1[:]))
-        prepare_w1(0, 0, "scalar")
-        w2_c = kept([P, PASSES, PASSES, PACK, P], U16, "w2_c")
-        nc.scalar.copy(
-            out=w2_c[:].rearrange("p g a i m -> p (g a) m i"),
-            in_=w2_raw[:].rearrange("p g n -> p (g n)").bitcast(U16).rearrange("p (q m i) -> p q m i", m=P, i=PACK),
-        )
-        gather_words(v_w[1], tabw[1], o1)
-        pages.extend([load_page(6), load_page(7)])
-        wgs_sb.append(load_wgs(CHUNKS[2][0], CHUNKS[2][1], "wgs2"))
-        tab2w[1] = load_words(tab2_words, 1, "tab2w1", "words3")
-        prepare_w1(0, 1, "scalar")
+        gather_words(v_w[0], tab_w[0], idx)
+        nc.vector.tensor_copy(v_s[:], tab_s[:].indirect(idx[:]))
+        quantise_w1(0, 0, nc.scalar.copy)
+        quantise_w1(0, 1, nc.scalar.copy)
         w2_s = kept([P, PASSES, PASSES, PACK, P], U8, "w2_s")
         nc.vector.tensor_copy(
             out=w2_s[:].rearrange("p g a i m -> p (g a) m i"),
             in_=w2_s_raw[:].rearrange("p g (a m i) -> p (g a) m i", a=PASSES, i=PACK),
         )
+        gather_words(v_w[1], tab_w[1], idx)
+        w2_c = kept([P, PASSES, PASSES, PACK, P], U16, "w2_c")
+        w2_raw_words = w2_raw[:].rearrange("p g n -> p (g n)").bitcast(U16)
+        nc.scalar.copy(
+            out=w2_c[:].rearrange("p g a i m -> p (g a) m i"),
+            in_=w2_raw_words.rearrange("p (q m i) -> p q m i", m=P, i=PACK),
+        )
+        pages.extend([load_page(k) for k in range(OWN_PAGE_BUFFERS, ROW_TILES)])
+        load_wgs(1, (0, 2, 1, 3))
+        tab2_w[1] = load_words(tab2_words, 1, "tab2_w1", "words3")
+        load_wgs(2, (0, 2, 1, 3))
+        nc.sync.dma_start(idx4[:], offs4)
+        gx_sb = load_channel_vector(gx, "gx_sb")
+        v2_s = kept([P, S2], U8, "v2_s")
+        nc.vector.tensor_copy(v2_s[:], tab2_s[:].indirect(idx2[:]))
+        quantise_w1(1, 0, nc.scalar.copy)
+        quantise_w1(1, 1, nc.vector.tensor_copy)
 
-        prepare_w1(1, 0, "scalar")
-        prepare_w1(1, 1, "vector")
-
-        t_sb = {}
+        tanh_sb = {}
+        d_grouped = {}
         d_c = {}
         d_s = {}
+        last = len(CHUNKS) - 1
 
         def features(c, a):
             c0, n = CHUNKS[c]
             cols = slice(c0, c0 + n)
-            if c == 2:
-                t = shared([P, PACK, n], F32, "t%d%d" % (c, a), "big%d" % a)
+            if c == last:
+                th = shared([P, PACK, n], F32, "tanh%d%d" % (c, a), "big%d" % a)
             else:
-                t = kept([P, PACK, n], F32, "t%d%d" % (c, a))
-            t_sb[c, a] = t
-            grouped = shared([P, n, PACK], BF16, "dg%d%d" % (c, a), "dg%d%d" % ((c + 2) % 3, a))
-            on_vector = c == 0 and a == 1
-            if not on_vector:
+                th = kept([P, PACK, n], F32, "tanh%d%d" % (c, a))
+            tanh_sb[c, a] = th
+            tag = "grouped%d%d" % ((c + last) % len(CHUNKS), a)
+            grouped = shared([P, n, PACK], BF16, "dg%d%d" % (c, a), tag)
+            if c > 0:
                 planes = shared([P, PACK, n], BF16, "dp%d%d" % (c, a), "planes")
             for i in range(PACK):
-                y1 = psum.tile([P, n], F32, name="y1_%d%d%d" % (c, a, i), tag="acc_a", bufs=3)
+                y1 = first_bank([P, n], "y1_%d%d%d" % (c, a, i))
                 for g in range(PASSES):
                     nc.tensor.matmul_mx(
                         out=y1[:],
@@ -209,35 +238,43 @@ def tile_list_log_cause_scores_kernel(
                         start=(g == 0),
                         stop=(g == PASSES - 1),
                     )
-                nc.scalar.activation(out=t[:, i, :], in_=y1[:], func=TANH, bias=b1_sb[:, a, i : i + 1])
-                if on_vector:
+                nc.scalar.activation(
+                    out=th[:, i, :], in_=y1[:], func=TANH, bias=b1_sb[:, a, i : i + 1]
+                )
+                if c == 0:
                     nc.vector.tensor_scalar(
-                        out=grouped[:, :, i], in0=t[:, i, :], scalar1=gd_sb[:, a, i : i + 1],
+                        out=grouped[:, :, i], in0=th[:, i, :], scalar1=gd_sb[:, a, i : i + 1],
                         scalar2=None, op0=MULT,
                     )
                 else:
                     nc.scalar.activation(
-                        out=planes[:, i, :], in_=t[:, i, :], func=COPY, scale=gd_sb[:, a, i : i + 1]
+                        out=planes[:, i, :], in_=th[:, i, :], func=COPY,
+                        scale=gd_sb[:, a, i : i + 1],
                     )
-            if not on_vector:
+            if c > 0:
                 nc.scalar.copy(
-                    out=grouped[:].rearrange("p (c e) i -> p c i e", e=4),
-                    in_=planes[:].rearrange("p i (c e) -> p c i e", e=4),
+                    out=grouped[:].rearrange("p (u e) i -> p u i e", e=4),
+                    in_=planes[:].rearrange("p i (u e) -> p u i e", e=4),
                 )
-            d_c[c, a] = kept([P, n], U32, "dc%d%d" % (c, a))
+            d_grouped[c, a] = grouped
+
+        def quantise_d(c, a, tag):
+            n = CHUNKS[c][1]
+            d_c[c, a] = shared([P, n], U32, "dc%d%d" % (c, a), tag)
             d_s[c, a] = kept([P, n], U8, "ds%d%d" % (c, a))
             nc.vector.quantize_mx(
                 out=d_c[c, a][:].bitcast(FP8X4),
                 scales=d_s[c, a][:],
-                in_=grouped[:].rearrange("p n i -> p (n i)"),
+                in_=d_grouped[c, a][:].rearrange("p n i -> p (n i)"),
             )
 
         h_sb = {}
 
         def mixture(c, k):
             a, i = divmod(k, PACK)
-            c0, n = CHUNKS[c]
-            y2 = psum.tile([P, n], F32, name="y2_%d%d" % (c, k), tag="acc_b", bufs=5)
+            n = CHUNKS[c][1]
+            bank = first_bank if c == 0 and k < FIRST_BANKS else second_bank
+            y2 = bank([P, n], "y2_%d%d" % (c, k))
             for g in range(PASSES):
                 nc.tensor.matmul_mx(
                     out=y2[:],
@@ -248,73 +285,84 @@ def tile_list_log_cause_scores_kernel(
                     start=(g == 0),
                     stop=(g == PASSES - 1),
                 )
-            gained = shared([P, n], F32, "h%d%d" % (c, k), "h", bufs=4)
-            nc.scalar.activation(out=gained[:], in_=y2[:], func=COPY, scale=gd_sb[:, a, i : i + 1])
-            h = t_sb[c, a][:, i, :]
-            nc.gpsimd.tensor_tensor(h, h, wgs_sb[c][:, i, :], MULT)
-            nc.gpsimd.tensor_tensor(h, h, gained[:], MULT)
+            if (c, k) in QUANTISE_AFTER or (c, k) == GATHER_AFTER:
+                h = shared([P, n], F32, "h%d%d" % (c, k), "h%d%d" % (c, k))
+            else:
+                h = shared([P, n], F32, "h%d%d" % (c, k), "h", bufs=RING)
+            nc.vector.scalar_tensor_tensor(
+                out=h[:], in0=y2[:], scalar=gd_sb[:, a, i : i + 1], in1=tanh_sb[c, a][:, i, :],
+                op0=MULT, op1=MULT,
+            )
             h_sb[c, k] = h
 
         def put(c, k):
             c0, n = CHUNKS[c]
-            nc.vector.tensor_copy(pages[k][:].indirect(o3[:, c0 // 16 : (c0 + n) // 16]), h_sb[c, k])
+            nc.vector.tensor_tensor(
+                pages[k][:].indirect(entries(idx3, c0, n)), h_sb[c, k][:],
+                wgs_sb[c][:, k % PACK, :], MULT,
+            )
 
-        x_g = {}
+        x_grouped = {}
         x_c = {}
         x_s = {}
 
         def fetch(k, j0, n):
             a, i = divmod(k, PACK)
-            picked = shared([P, n], F32, "picked%d_%d" % (k, j0), "picked", bufs=3)
-            nc.vector.tensor_copy(picked[:], pages[k][:].indirect(o4[:, j0 // 16 : (j0 + n) // 16]))
-            if a not in x_g:
-                x_g[a] = shared([P, NP, PACK], BF16, "xg%d" % a, "dg1%d" % a)
+            picked = shared([P, n], F32, "picked%d_%d" % (k, j0), "picked", bufs=RING)
+            nc.vector.tensor_copy(picked[:], pages[k][:].indirect(entries(idx4, j0, n)))
+            if a not in x_grouped:
+                x_grouped[a] = shared([P, NP, PACK], BF16, "xg%d" % a, "grouped1%d" % a)
                 x_c[a] = shared([P, NP], U32, "xc%d" % a, "code%d" % a)
                 x_s[a] = kept([P, NP], U8, "xs%d" % a)
             nc.scalar.activation(
-                out=x_g[a][:, j0 : j0 + n, i], in_=picked[:], func=COPY, scale=gx_sb[:, a, i : i + 1]
+                out=x_grouped[a][:, j0 : j0 + n, i], in_=picked[:], func=COPY,
+                scale=gx_sb[:, a, i : i + 1],
             )
 
         def quantise_x(a, j0, n):
             nc.vector.quantize_mx(
                 out=x_c[a][:, j0 : j0 + n].bitcast(FP8X4),
                 scales=x_s[a][:, j0 : j0 + n],
-                in_=x_g[a][:, j0 : j0 + n, :].rearrange("p n i -> p (n i)"),
+                in_=x_grouped[a][:, j0 : j0 + n, :].rearrange("p n i -> p (n i)"),
             )
 
-        features(0, 0)
-        features(0, 1)
-        v2_s = shared([P, S2], U8, "v2_s", "bf1")
-        nc.vector.tensor_copy(v2_s[:], tab2_s[:].indirect(o2[:]))
-        v2_w[0] = shared([P, S2], U32, "v2_w0", "dg21")
-        gather_words(v2_w[0], tab2w[0], o2)
-        steps = [(c, k) for half in range(2) for c in range(2) for k in range(PACK * half, PACK * (half + 1))]
-        steps.extend([(c, k) for c in range(2, len(CHUNKS)) for k in range(8)])
-        last = len(CHUNKS) - 1
+        for a in range(PASSES):
+            features(0, a)
+            quantise_d(0, a, "dc0%d" % a)
+        v2_w[0] = shared([P, S2], U32, "v2_w0", "bf1")
+        gather_words(v2_w[0], tab2_w[0], idx2)
+        steps = [(c, k) for c in range(len(CHUNKS)) for k in range(ROW_TILES)]
+        for k in range(FIRST_BANKS):
+            mixture(0, k)
+        for c in range(1, len(CHUNKS)):
+            for a in range(PASSES):
+                features(c, a)
         for s, (c, k) in enumerate(steps):
-            if c > 0 and k == 0:
-                features(c, 0)
-                features(c, 1)
-            mixture(c, k)
+            if FIRST_BANKS <= s + 1 < len(steps):
+                mixture(*steps[s + 1])
             put(c, k)
-            if s == 16:
-                gather_words(v2_w[1], tab2w[1], o2)
-                topo_sb = [load_topo(0), load_topo(1)]
+            if (c, k) in QUANTISE_AFTER:
+                quantise_d(*QUANTISE_AFTER[c, k], "h%d%d" % (c, k))
+            if (c, k) == GATHER_AFTER:
+                v2_w[1] = shared([P, S2], U32, "v2_w1", "h%d%d" % (c, k))
+                gather_words(v2_w[1], tab2_w[1], idx2)
+                topo_sb = [load_topo(half) for half in range(2)]
             if c == last and k > 0:
                 fetch(k - 1, 0, NP)
             if c == last and k == PACK + 1:
                 quantise_x(0, 0, NP)
+
         half_p = NP // 2
         for jh in range(2):
-            fetch(7, half_p * jh, half_p)
+            fetch(ROW_TILES - 1, half_p * jh, half_p)
         for jh in range(2):
-            quantise_x(1, half_p * jh, half_p)
+            quantise_x(PASSES - 1, half_p * jh, half_p)
 
-        banks = [(jh, mp) for jh in range(2) for mp in range(4)]
+        banks = [(jh, mp) for jh in range(2) for mp in range(S2 // (2 * P))]
         acc = {}
         for b, key in enumerate(banks):
-            tag, bufs = ("acc_a", 3) if b < 3 else ("acc_b", 5)
-            acc[key] = psum.tile([P, 2, half_p], F32, name="e%d" % b, tag=tag, bufs=bufs)
+            bank = first_bank if b < FIRST_BANKS else second_bank
+            acc[key] = bank([P, 2, half_p], "e%d" % b)
         for g in range(PASSES):
             for jh, mp in banks:
                 cols = slice(half_p * jh, half_p * (jh + 1))
@@ -329,15 +377,14 @@ def tile_list_log_cause_scores_kernel(
                         start=(g == 0 and u == 0),
                         stop=(g == PASSES - 1 and u == 1),
                     )
-        res = [shared([P, 4, 2, half_p], F32, "res%d" % jh, "big%d" % (2 + jh)) for jh in range(2)]
+        res = [
+            shared([P, S2 // (2 * P), 2, half_p], F32, "res%d" % jh, "big%d" % (2 + jh))
+            for jh in range(2)
+        ]
         out_rows = out.rearrange("(t p) j -> p t j", p=P)
         for jh, mp in banks:
             cols = slice(half_p * jh, half_p * (jh + 1))
-            r = res[jh][:, mp, :, :]
+            scores = res[jh][:, mp, :, :]
             given = topo_sb[mp // 2][:, 2 * (mp % 2) : 2 * (mp % 2) + 2, cols]
-            if jh == 0 and mp % 2 == 1:
-                nc.scalar.copy(out=r, in_=acc[jh, mp][:])
-                nc.gpsimd.tensor_tensor(r, r, given, ADD)
-            else:
-                nc.vector.tensor_tensor(r, acc[jh, mp][:], given, ADD)
-            nc.sync.dma_start(out=out_rows[:, 2 * mp : 2 * mp + 2, cols], in_=r)
+            nc.vector.tensor_tensor(scores, acc[jh, mp][:], given, ADD)
+            nc.sync.dma_start(out=out_rows[:, 2 * mp : 2 * mp + 2, cols], in_=scores)

from contextlib import ExitStack

import concourse.mybir as mybir

K, H, T, S, T2, T3, S2, NP = 1024, 1024, 2048, 1024, 2048, 2048, 1024, 512
FLOPS = 2 * K * H * S + 2 * H * H * S + 2 * H * S2 * NP

F32 = mybir.dt.float32
BF16 = mybir.dt.bfloat16
I32 = mybir.dt.int32
U32 = mybir.dt.uint32
U16 = mybir.dt.uint16
U8 = mybir.dt.uint8
FP8X4 = mybir.dt.float8_e4m3fn_x4
FP4X4 = mybir.dt.float4_e2m1fn_x4
MULT = mybir.AluOpType.mult
ADD = mybir.AluOpType.add
COPY = mybir.ActivationFunctionType.Copy
TANH = mybir.ActivationFunctionType.Tanh

P = 128
PACK = 4
KP = P * PACK
PASSES = 2
ROW_TILES = PASSES * PACK
QUADRANTS = 4
LIST_GROUP = 16

CHUNKS = ((0, 256), (256, 256), (512, 512))
QUANTISE_AFTER = {(0, 3): (1, 0), (0, 5): (1, 1), (1, 2): (2, 0), (1, 5): (2, 1)}
GATHER_AFTER = (1, 3)
FIRST_BANKS = 3
SECOND_BANKS = 5
RING = 3
OWN_PAGE_BUFFERS = 6


def tile_list_log_cause_scores_kernel(
    tc, tab_words, tab_scales, tab2_words, tab2_scales, offs, offs2, offs3, offs4,
    w1, b1, gd, w2_words, w2_scales, wgs, page0, gx, topo, out,
):
    nc = tc.nc
    with ExitStack() as ctx:
        keep = ctx.enter_context(tc.tile_pool(name="keep", bufs=1))
        ring = ctx.enter_context(tc.tile_pool(name="ring", bufs=1))
        psum = ctx.enter_context(tc.psum_pool(name="psum", bufs=1))

        def kept(shape, dtype, name):
            return keep.tile(shape, dtype, name=name, align_bytes=64)

        def shared(shape, dtype, name, tag, bufs=1):
            return ring.tile(shape, dtype, name=name, tag=tag, bufs=bufs, align_bytes=64)

        def first_bank(shape, name):
            return psum.tile(shape, F32, name=name, tag="acc_a", bufs=FIRST_BANKS)

        def second_bank(shape, name):
            return psum.tile(shape, F32, name=name, tag="acc_b", bufs=SECOND_BANKS)

        idx = keep.tile([P, S // LIST_GROUP], U16, name="idx")
        idx2 = keep.tile([P, S2 // LIST_GROUP], U16, name="idx2")
        idx3 = keep.tile([P, S // LIST_GROUP], U16, name="idx3")
        idx4 = keep.tile([P, NP // LIST_GROUP], U16, name="idx4")

        def entries(list_tile, j0, n):
            return list_tile[:, j0 // LIST_GROUP : (j0 + n) // LIST_GROUP]

        tab_s = kept([P, T], U8, "tab_s")
        tab2_s = kept([P, T3], U8, "tab2_s")
        w2_s_raw = shared([P, PASSES, H], U8, "w2_s_raw", "picked", bufs=RING)
        nc.gpsimd.memset(tab_s[:].bitcast(I32), 0)
        nc.vector.memset(w2_s_raw[:].rearrange("p g n -> p (g n)").bitcast(I32), 0)
        nc.vector.memset(tab2_s[:].bitcast(I32), 0)

        def load_table_scales(tile, src, quadrants):
            for q in quadrants:
                nc.sync.dma_start(
                    out=tile[32 * q : 32 * q + 4 * PASSES, :].bitcast(I32),
                    in_=src[:, 4 * q : 4 * q + 4, :].bitcast(I32),
                )

        def load_words(src, g, name, tag):
            words = shared([P, T], I32, name, tag)
            nc.sync.dma_start(out=words[:], in_=src[g].rearrange("p t i -> p (t i)").bitcast(I32))
            return words

        def load_w1(g, c0, width, tag):
            raw = shared([P, PACK, width], F32, "w1raw%d_%d" % (g, c0), tag)
            rows = w1[KP * g : KP * (g + 1), c0 : c0 + width]
            nc.sync.dma_start(out=raw[:], in_=rows.rearrange("(p j) c -> p j c", j=PACK))
            return raw

        def load_channel_vector(src, name):
            vec = kept([P, PASSES, PACK], F32, name)
            nc.sync.dma_start(out=vec[:], in_=src.rearrange("(a p i) -> p a i", a=PASSES, i=PACK))
            return vec

        def load_wgs(c, quadrants):
            c0, n = CHUNKS[c]
            for q in quadrants:
                nc.sync.dma_start(
                    out=wgs_sb[c][32 * q : 32 * q + 32, :, :],
                    in_=wgs[:, c0 : c0 + n].rearrange("(p i) j -> p i j", i=PACK),
                )

        page_rows = page0.rearrange("(a p i) c -> a i p c", a=PASSES, i=PACK)

        def load_page(k):
            tag = "page%d" % k if k < OWN_PAGE_BUFFERS else "words%d" % (k - OWN_PAGE_BUFFERS)
            page = shared([P, T2], F32, "page%d" % k, tag)
            nc.sync.dma_start(out=page[:], in_=page_rows[k // PACK, k % PACK])
            return page

        def load_topo(half):
            rows = shared([P, PACK, NP], F32, "topo%d" % half, "words%d" % (PASSES + half))
            nc.sync.dma_start(
                out=rows[:],
                in_=topo[KP * half : KP * (half + 1), :].rearrange("(t p) j -> p t j", p=P),
            )
            return rows

        tab_w = {}
        tab2_w = {}
        w1raw = {}
        nc.sync.dma_start(idx[:], offs)
        tab_w[0] = load_words(tab_words, 0, "tab_w0", "words0")
        b1_sb = load_channel_vector(b1, "b1_sb")
        gd_sb = load_channel_vector(gd, "gd_sb")
        load_table_scales(tab_s, tab_scales, range(QUADRANTS))
        w1raw[0, 0] = [load_w1(0, 0, KP, "big0")]
        w1raw[0, 1] = [load_w1(1, 0, KP, "big1")]
        for q in range(QUADRANTS):
            nc.sync.dma_start(
                out=w2_s_raw[32 * q : 32 * q + 4, :, :].bitcast(I32),
                in_=w2_scales[:, 4 * q : 4 * q + 4, :].rearrange("g r n -> r g n").bitcast(I32),
            )
        tab_w[1] = load_words(tab_words, 1, "tab_w1", "words1")
        nc.sync.dma_start(idx2[:], offs2)
        load_table_scales(tab2_s, tab2_scales, (0, 1))
        w2_raw = shared([P, PASSES, 2 * H], U8, "w2_raw", "grouped10")
        nc.sync.dma_start(
            out=w2_raw[:].bitcast(I32), in_=w2_words.rearrange("g p n -> p g n").bitcast(I32)
        )
        load_table_scales(tab2_s, tab2_scales, (2, 3))
        w1raw[1, 0] = [load_w1(0, KP, KP, "big2")]
        nc.sync.dma_start(idx3[:], offs3)
        w1raw[1, 1] = [
            load_w1(1, KP + u * (KP // 2), KP // 2, tag) for u, tag in enumerate(("big3", "planes"))
        ]
        wgs_sb = [kept([P, PACK, n], F32, "wgs%d" % c0) for c0, n in CHUNKS]
        load_wgs(0, (0, 2))
        tab2_w[0] = load_words(tab2_words, 0, "tab2_w0", "words2")
        load_wgs(0, (1, 3))
        pages = [load_page(k) for k in range(OWN_PAGE_BUFFERS)]

        v_s = kept([P, S], U8, "v_s")
        v_w = [kept([P, S], U32, "v_w%d" % g) for g in range(PASSES)]
        v2_w = {}

        def gather_words(dst, src, list_tile):
            nc.vector.tensor_copy(dst[:], src[:].bitcast(U32).indirect(list_tile[:]))

        w1_c = {}
        w1_s = {}

        def quantise_w1(a, g, cast):
            dealt = shared([P, PACK, P, PACK], BF16, "w1bf%d%d" % (a, g), "bf%d" % g)
            walk = dealt[:].rearrange("p i m j -> p m j i")
            pieces = w1raw[a, g]
            width = P // len(pieces)
            for u, raw in enumerate(pieces):
                cast(
                    out=walk[:, u * width : (u + 1) * width],
                    in_=raw[:].rearrange("p j (m i) -> p m j i", i=PACK),
                )
            w1_c[a, g] = shared([P, KP], U32, "w1c%d%d" % (a, g), "code%d" % (PASSES * a + g))
            w1_s[a, g] = kept([P, KP], U8, "w1s%d%d" % (a, g))
            nc.vector.quantize_mx(
                out=w1_c[a, g][:].bitcast(FP8X4),
                scales=w1_s[a, g][:],
                in_=dealt[:].rearrange("p i m j -> p (i m j)"),
            )

        gather_words(v_w[0], tab_w[0], idx)
        nc.vector.tensor_copy(v_s[:], tab_s[:].indirect(idx[:]))
        quantise_w1(0, 0, nc.scalar.copy)
        quantise_w1(0, 1, nc.scalar.copy)
        w2_s = kept([P, PASSES, PASSES, PACK, P], U8, "w2_s")
        nc.vector.tensor_copy(
            out=w2_s[:].rearrange("p g a i m -> p (g a) m i"),
            in_=w2_s_raw[:].rearrange("p g (a m i) -> p (g a) m i", a=PASSES, i=PACK),
        )
        gather_words(v_w[1], tab_w[1], idx)
        w2_c = kept([P, PASSES, PASSES, PACK, P], U16, "w2_c")
        w2_raw_words = w2_raw[:].rearrange("p g n -> p (g n)").bitcast(U16)
        nc.scalar.copy(
            out=w2_c[:].rearrange("p g a i m -> p (g a) m i"),
            in_=w2_raw_words.rearrange("p (q m i) -> p q m i", m=P, i=PACK),
        )
        pages.extend([load_page(k) for k in range(OWN_PAGE_BUFFERS, ROW_TILES)])
        load_wgs(1, (0, 2, 1, 3))
        tab2_w[1] = load_words(tab2_words, 1, "tab2_w1", "words3")
        load_wgs(2, (0, 2, 1, 3))
        nc.sync.dma_start(idx4[:], offs4)
        gx_sb = load_channel_vector(gx, "gx_sb")
        v2_s = kept([P, S2], U8, "v2_s")
        nc.vector.tensor_copy(v2_s[:], tab2_s[:].indirect(idx2[:]))
        quantise_w1(1, 0, nc.scalar.copy)
        quantise_w1(1, 1, nc.vector.tensor_copy)

        tanh_sb = {}
        d_grouped = {}
        d_c = {}
        d_s = {}
        last = len(CHUNKS) - 1

        def features(c, a):
            c0, n = CHUNKS[c]
            cols = slice(c0, c0 + n)
            if c == last:
                th = shared([P, PACK, n], F32, "tanh%d%d" % (c, a), "big%d" % a)
            else:
                th = kept([P, PACK, n], F32, "tanh%d%d" % (c, a))
            tanh_sb[c, a] = th
            tag = "grouped%d%d" % ((c + last) % len(CHUNKS), a)
            grouped = shared([P, n, PACK], BF16, "dg%d%d" % (c, a), tag)
            if c > 0:
                planes = shared([P, PACK, n], BF16, "dp%d%d" % (c, a), "planes")
            for i in range(PACK):
                y1 = first_bank([P, n], "y1_%d%d%d" % (c, a, i))
                for g in range(PASSES):
                    nc.tensor.matmul_mx(
                        out=y1[:],
                        lhsT=w1_c[a, g][:, P * i : P * (i + 1)].bitcast(FP8X4),
                        lhsT_scale=w1_s[a, g][:, P * i : P * (i + 1)],
                        rhs=v_w[g][:, cols].bitcast(FP8X4),
                        rhs_scale=v_s[4 * g : P, cols],
                        start=(g == 0),
                        stop=(g == PASSES - 1),
                    )
                nc.scalar.activation(
                    out=th[:, i, :], in_=y1[:], func=TANH, bias=b1_sb[:, a, i : i + 1]
                )
                if c == 0:
                    nc.vector.tensor_scalar(
                        out=grouped[:, :, i], in0=th[:, i, :], scalar1=gd_sb[:, a, i : i + 1],
                        scalar2=None, op0=MULT,
                    )
                else:
                    nc.scalar.activation(
                        out=planes[:, i, :], in_=th[:, i, :], func=COPY,
                        scale=gd_sb[:, a, i : i + 1],
                    )
            if c > 0:
                nc.scalar.copy(
                    out=grouped[:].rearrange("p (u e) i -> p u i e", e=4),
                    in_=planes[:].rearrange("p i (u e) -> p u i e", e=4),
                )
            d_grouped[c, a] = grouped

        def quantise_d(c, a, tag):
            n = CHUNKS[c][1]
            d_c[c, a] = shared([P, n], U32, "dc%d%d" % (c, a), tag)
            d_s[c, a] = kept([P, n], U8, "ds%d%d" % (c, a))
            nc.vector.quantize_mx(
                out=d_c[c, a][:].bitcast(FP8X4),
                scales=d_s[c, a][:],
                in_=d_grouped[c, a][:].rearrange("p n i -> p (n i)"),
            )

        h_sb = {}

        def mixture(c, k):
            a, i = divmod(k, PACK)
            n = CHUNKS[c][1]
            bank = first_bank if c == 0 and k < FIRST_BANKS else second_bank
            y2 = bank([P, n], "y2_%d%d" % (c, k))
            for g in range(PASSES):
                nc.tensor.matmul_mx(
                    out=y2[:],
                    lhsT=w2_c[:, g, a, i, :].bitcast(FP4X4),
                    lhsT_scale=w2_s[:, g, a, i, :],
                    rhs=d_c[c, g][:].bitcast(FP8X4),
                    rhs_scale=d_s[c, g][:],
                    start=(g == 0),
                    stop=(g == PASSES - 1),
                )
            if (c, k) in QUANTISE_AFTER or (c, k) == GATHER_AFTER:
                h = shared([P, n], F32, "h%d%d" % (c, k), "h%d%d" % (c, k))
            else:
                h = shared([P, n], F32, "h%d%d" % (c, k), "h", bufs=RING)
            nc.vector.scalar_tensor_tensor(
                out=h[:], in0=y2[:], scalar=gd_sb[:, a, i : i + 1], in1=tanh_sb[c, a][:, i, :],
                op0=MULT, op1=MULT,
            )
            h_sb[c, k] = h

        def put(c, k):
            c0, n = CHUNKS[c]
            nc.vector.tensor_tensor(
                pages[k][:].indirect(entries(idx3, c0, n)), h_sb[c, k][:],
                wgs_sb[c][:, k % PACK, :], MULT,
            )

        x_grouped = {}
        x_c = {}
        x_s = {}

        def fetch(k, j0, n):
            a, i = divmod(k, PACK)
            picked = shared([P, n], F32, "picked%d_%d" % (k, j0), "picked", bufs=RING)
            nc.vector.tensor_copy(picked[:], pages[k][:].indirect(entries(idx4, j0, n)))
            if a not in x_grouped:
                x_grouped[a] = shared([P, NP, PACK], BF16, "xg%d" % a, "grouped1%d" % a)
                x_c[a] = shared([P, NP], U32, "xc%d" % a, "code%d" % a)
                x_s[a] = kept([P, NP], U8, "xs%d" % a)
            nc.scalar.activation(
                out=x_grouped[a][:, j0 : j0 + n, i], in_=picked[:], func=COPY,
                scale=gx_sb[:, a, i : i + 1],
            )

        def quantise_x(a, j0, n):
            nc.vector.quantize_mx(
                out=x_c[a][:, j0 : j0 + n].bitcast(FP8X4),
                scales=x_s[a][:, j0 : j0 + n],
                in_=x_grouped[a][:, j0 : j0 + n, :].rearrange("p n i -> p (n i)"),
            )

        for a in range(PASSES):
            features(0, a)
            quantise_d(0, a, "dc0%d" % a)
        v2_w[0] = shared([P, S2], U32, "v2_w0", "bf1")
        gather_words(v2_w[0], tab2_w[0], idx2)
        steps = [(c, k) for c in range(len(CHUNKS)) for k in range(ROW_TILES)]
        for k in range(FIRST_BANKS):
            mixture(0, k)
        for c in range(1, len(CHUNKS)):
            for a in range(PASSES):
                features(c, a)
        for s, (c, k) in enumerate(steps):
            if FIRST_BANKS <= s + 1 < len(steps):
                mixture(*steps[s + 1])
            put(c, k)
            if (c, k) in QUANTISE_AFTER:
                quantise_d(*QUANTISE_AFTER[c, k], "h%d%d" % (c, k))
            if (c, k) == GATHER_AFTER:
                v2_w[1] = shared([P, S2], U32, "v2_w1", "h%d%d" % (c, k))
                gather_words(v2_w[1], tab2_w[1], idx2)
                topo_sb = [load_topo(half) for half in range(2)]
            if c == last and k > 0:
                fetch(k - 1, 0, NP)
            if c == last and k == PACK + 1:
                quantise_x(0, 0, NP)

        half_p = NP // 2
        for jh in range(2):
            fetch(ROW_TILES - 1, half_p * jh, half_p)
        for jh in range(2):
            quantise_x(PASSES - 1, half_p * jh, half_p)

        banks = [(jh, mp) for jh in range(2) for mp in range(S2 // (2 * P))]
        acc = {}
        for b, key in enumerate(banks):
            bank = first_bank if b < FIRST_BANKS else second_bank
            acc[key] = bank([P, 2, half_p], "e%d" % b)
        for g in range(PASSES):
            for jh, mp in banks:
                cols = slice(half_p * jh, half_p * (jh + 1))
                for u in range(2):
                    m = 2 * mp + u
                    nc.tensor.matmul_mx(
                        out=acc[jh, mp][:, u, :],
                        lhsT=v2_w[g][:, P * m : P * (m + 1)].bitcast(FP8X4),
                        lhsT_scale=v2_s[4 * g : P, P * m : P * (m + 1)],
                        rhs=x_c[g][:, cols].bitcast(FP8X4),
                        rhs_scale=x_s[g][:, cols],
                        start=(g == 0 and u == 0),
                        stop=(g == PASSES - 1 and u == 1),
                    )
        res = [
            shared([P, S2 // (2 * P), 2, half_p], F32, "res%d" % jh, "big%d" % (2 + jh))
            for jh in range(2)
        ]
        out_rows = out.rearrange("(t p) j -> p t j", p=P)
        for jh, mp in banks:
            cols = slice(half_p * jh, half_p * (jh + 1))
            scores = res[jh][:, mp, :, :]
            given = topo_sb[mp // 2][:, 2 * (mp % 2) : 2 * (mp % 2) + 2, cols]
            nc.vector.tensor_tensor(scores, acc[jh, mp][:], given, ADD)
            nc.sync.dma_start(out=out_rows[:, 2 * mp : 2 * mp + 2, cols], in_=scores)
